import numpy as np
CORES = [6,14,22,30,38,46,54,62,134,142,150,158,166,174,182,190,262,270,278,286,294,302,310,318,390,398,406,414,422,430,438,446]
N = 32
def setup_inputs(rng):
    return {"x": rng.standard_normal((N, 128, 32), dtype=np.float32)}
def reference(x):
    s = x.sum(axis=0, dtype=np.float64).astype(x.dtype)
    b = 32 // N
    return {"y": np.stack([s[:, r * b:(r + 1) * b] for r in range(N)])}

@@ -1,0 +1,47 @@
+from concourse.bass import DstId, RemoteDMATransfer
+
+SCRATCH = {
+    "xs": ("sbuf", [128, 32], "float32"),
+    "cab": ("sbuf", [128, 16], "float32"),
+    "land": ("sbuf", [128, 16], "float32"),
+    "res": ("sbuf", [128, 1], "float32"),
+}
+SEMAPHORES = ["loaded", "sent", "cabarr", "arrived", "done", "stored"]
+
+
+def rank_program(g, core, T, topo):
+    h, c, k = topo.host(core), topo.chip(core), core % 8
+    if c >= 8 or k not in (6, 7):
+        return
+    if k == 7:
+        g.wait_ge(T.sem.arrived, 16)
+        rid, pid = topo.addr(core - 1, core)
+        g.remote_dma_fused([RemoteDMATransfer(
+            dst_ids=[DstId(rid=rid, pnc=pid)], dma_engine_mask=0xFFFF, remote_sem=T.sem.done,
+            srcs=[T.land[:, s:s + 1] for s in range(16)], dsts=[T.res[:, :]], alu_op=1)], local_sem=T.sem.sent)
+        g.wait_ge(T.sem.sent, 16)
+        return
+    R = topo.rack(h)
+    g.dma_start(T.xs[:, :], T.x[:, :]).then_inc(T.sem.loaded, 16)
+    g.wait_ge(T.sem.loaded, 16)
+    far = (3 - h) * 128 + c * 8 + 6
+    rid, pid = topo.addr(far, core)
+    o = 16 * (1 - R)
+    g.remote_dma(T.cab[:, :], T.xs[:, o:o + 16], T.sem.cabarr, T.sem.sent, pid, rid, 0xFF)
+    g.wait_ge(T.sem.cabarr, 8)
+    slot = (h - 2 * R) * 8 + c
+    for half in range(2):
+        trs = []
+        for e in range(8):
+            jl = half * 8 + e
+            d = (2 * R + half) * 128 + e * 8 + 7
+            rid, pid = topo.addr(d, core)
+            trs.append(RemoteDMATransfer(
+                dst_ids=[DstId(rid=rid, pnc=pid)], dma_engine_mask=1 << e, remote_sem=T.sem.arrived,
+                srcs=[T.xs[:, 16 * R + jl:16 * R + jl + 1], T.cab[:, jl:jl + 1]],
+                dsts=[T.land[:, slot:slot + 1]], alu_op=1))
+        g.remote_dma_fused(trs, local_sem=T.sem.sent)
+    g.wait_ge(T.sem.done, 16)
+    g.dma_start(T.y[:, :], T.res[:, :]).then_inc(T.sem.stored, 16)
+    g.wait_ge(T.sem.sent, 24)
+    g.wait_ge(T.sem.stored, 16)

@@ -1,47 +1,61 @@
 from concourse.bass import DstId, RemoteDMATransfer
 
 SCRATCH = {
-    "xs": ("sbuf", [128, 32], "float32"),
-    "cab": ("sbuf", [128, 16], "float32"),
-    "land": ("sbuf", [128, 16], "float32"),
-    "res": ("sbuf", [128, 1], "float32"),
+    "xd": ("dram", [2, 16, 128, 1], "float32"),
+    "landf": ("dram", [16, 128, 1], "float32"),
+    "lando": ("dram", [16, 128, 1], "float32"),
+    "cabl": ("dram", [128, 1], "float32"),
+    "gath": ("dram", [16, 128, 1], "float32"),
 }
-SEMAPHORES = ["loaded", "sent", "cabarr", "arrived", "done", "stored"]
+SEMAPHORES = ["ldf", "ldo", "sent", "arrf", "arro", "cabarr", "gathd", "stored"]
+
+RANK_CORE, RED_CORE = 6, 2
+
+
+def _world(h, c, k):
+    return h * 128 + c * 8 + k
+
+
+def _hosts(R):
+    return (0, 1) if R == 0 else (3, 2)
 
 
 def rank_program(g, core, T, topo):
     h, c, k = topo.host(core), topo.chip(core), core % 8
-    if c >= 8 or k not in (6, 7):
-        return
-    if k == 7:
-        g.wait_ge(T.sem.arrived, 16)
-        rid, pid = topo.addr(core - 1, core)
-        g.remote_dma_fused([RemoteDMATransfer(
-            dst_ids=[DstId(rid=rid, pnc=pid)], dma_engine_mask=0xFFFF, remote_sem=T.sem.done,
-            srcs=[T.land[:, s:s + 1] for s in range(16)], dsts=[T.res[:, :]], alu_op=1)], local_sem=T.sem.sent)
-        g.wait_ge(T.sem.sent, 16)
+    if c >= 8 or k not in (RANK_CORE, RED_CORE):
         return
     R = topo.rack(h)
-    g.dma_start(T.xs[:, :], T.x[:, :]).then_inc(T.sem.loaded, 16)
-    g.wait_ge(T.sem.loaded, 16)
-    far = (3 - h) * 128 + c * 8 + 6
-    rid, pid = topo.addr(far, core)
-    o = 16 * (1 - R)
-    g.remote_dma(T.cab[:, :], T.xs[:, o:o + 16], T.sem.cabarr, T.sem.sent, pid, rid, 0xFF)
-    g.wait_ge(T.sem.cabarr, 8)
-    slot = (h - 2 * R) * 8 + c
-    for half in range(2):
-        trs = []
-        for e in range(8):
-            jl = half * 8 + e
-            d = (2 * R + half) * 128 + e * 8 + 7
-            rid, pid = topo.addr(d, core)
-            trs.append(RemoteDMATransfer(
-                dst_ids=[DstId(rid=rid, pnc=pid)], dma_engine_mask=1 << e, remote_sem=T.sem.arrived,
-                srcs=[T.xs[:, 16 * R + jl:16 * R + jl + 1], T.cab[:, jl:jl + 1]],
-                dsts=[T.land[:, slot:slot + 1]], alu_op=1))
-        g.remote_dma_fused(trs, local_sem=T.sem.sent)
-    g.wait_ge(T.sem.done, 16)
-    g.dma_start(T.y[:, :], T.res[:, :]).then_inc(T.sem.stored, 16)
-    g.wait_ge(T.sem.sent, 24)
+    hosts = _hosts(R)
+    me = hosts.index(h) * 8 + c
+
+    def dst(d):
+        rid, pid = topo.addr(d, core)
+        return DstId(rid=rid, pnc=pid)
+
+    if k == RED_CORE:
+        g.wait_ge(T.sem.arrf, 16)
+        g.remote_dma_fused([RemoteDMATransfer(
+            dst_ids=[dst(_world(3 - h, c, RED_CORE))], dma_engine_mask=0xFF, remote_sem=T.sem.cabarr,
+            srcs=[T.landf[s] for s in range(16)], dsts=[T.cabl[:, :]], alu_op=1)], local_sem=T.sem.sent)
+        g.wait_ge(T.sem.arro, 16)
+        g.wait_ge(T.sem.cabarr, 8)
+        srcs = [T.lando[s] for s in range(16)] + [T.cabl[:, :]]
+        g.remote_dma_fused([RemoteDMATransfer(
+            dst_ids=[dst(_world(hh, e, RANK_CORE)) for hh in hosts], dma_engine_mask=1 << e, remote_sem=T.sem.gathd,
+            srcs=srcs, dsts=[T.gath[me], T.gath[me]], alu_op=1) for e in range(8)], local_sem=T.sem.sent)
+        g.wait_ge(T.sem.sent, 16)
+        return
+
+    g.sync.dma_start(T.xd[1 - R], T.x[:, 16 * (1 - R):16 * (1 - R) + 16]).then_inc(T.sem.ldf, 16)
+    g.scalar.dma_start(T.xd[R], T.x[:, 16 * R:16 * R + 16]).then_inc(T.sem.ldo, 16)
+    for half, ld, buf, arr in ((1 - R, T.sem.ldf, T.landf, T.sem.arrf), (R, T.sem.ldo, T.lando, T.sem.arro)):
+        g.wait_ge(ld, 16)
+        for u in range(2):
+            g.remote_dma_fused([RemoteDMATransfer(
+                dst_ids=[dst(_world(hosts[u], e, RED_CORE))], dma_engine_mask=1 << e, remote_sem=arr,
+                src=T.xd[half, u * 8 + e], dst=buf[me]) for e in range(8)], local_sem=T.sem.sent)
+    g.wait_ge(T.sem.gathd, 16)
+    jl = (h * 8 + c) - 16 * R
+    g.dma_start(T.y[:, :], T.gath[:, jl::16, :], allow_slow_non_contiguous=True).then_inc(T.sem.stored, 16)
+    g.wait_ge(T.sem.sent, 32)
     g.wait_ge(T.sem.stored, 16)

@@ -2,14 +2,13 @@ from concourse.bass import DstId, RemoteDMATransfer
 
 SCRATCH = {
     "xd": ("dram", [2, 16, 128, 1], "float32"),
-    "landf": ("dram", [16, 128, 1], "float32"),
-    "lando": ("dram", [16, 128, 1], "float32"),
+    "land": ("dram", [16, 128, 1], "float32"),
     "cabl": ("dram", [128, 1], "float32"),
     "gath": ("dram", [16, 128, 1], "float32"),
 }
-SEMAPHORES = ["ldf", "ldo", "sent", "arrf", "arro", "cabarr", "gathd", "stored"]
+SEMAPHORES = ["ldf", "ldo", "sent", "arr", "cabarr", "gathd", "stored"]
 
-RANK_CORE, RED_CORE = 6, 2
+RANK_CORE, FWD_CORE, RED_CORE = 6, 7, 2
 
 
 def _world(h, c, k):
@@ -22,7 +21,7 @@ def _hosts(R):
 
 def rank_program(g, core, T, topo):
     h, c, k = topo.host(core), topo.chip(core), core % 8
-    if c >= 8 or k not in (RANK_CORE, RED_CORE):
+    if c >= 8 or k not in (RANK_CORE, FWD_CORE, RED_CORE):
         return
     R = topo.rack(h)
     hosts = _hosts(R)
@@ -32,28 +31,34 @@ def rank_program(g, core, T, topo):
         rid, pid = topo.addr(d, core)
         return DstId(rid=rid, pnc=pid)
 
-    if k == RED_CORE:
-        g.wait_ge(T.sem.arrf, 16)
+    landed = [T.land[s] for s in range(16)]
+
+    if k == FWD_CORE:
+        g.wait_ge(T.sem.arr, 16)
         g.remote_dma_fused([RemoteDMATransfer(
             dst_ids=[dst(_world(3 - h, c, RED_CORE))], dma_engine_mask=0xFF, remote_sem=T.sem.cabarr,
-            srcs=[T.landf[s] for s in range(16)], dsts=[T.cabl[:, :]], alu_op=1)], local_sem=T.sem.sent)
-        g.wait_ge(T.sem.arro, 16)
+            srcs=landed, dsts=[T.cabl[:, :]], alu_op=1)], local_sem=T.sem.sent)
+        g.wait_ge(T.sem.sent, 8)
+        return
+
+    if k == RED_CORE:
+        g.wait_ge(T.sem.arr, 16)
         g.wait_ge(T.sem.cabarr, 8)
-        srcs = [T.lando[s] for s in range(16)] + [T.cabl[:, :]]
         g.remote_dma_fused([RemoteDMATransfer(
             dst_ids=[dst(_world(hh, e, RANK_CORE)) for hh in hosts], dma_engine_mask=1 << e, remote_sem=T.sem.gathd,
-            srcs=srcs, dsts=[T.gath[me], T.gath[me]], alu_op=1) for e in range(8)], local_sem=T.sem.sent)
-        g.wait_ge(T.sem.sent, 16)
+            srcs=landed + [T.cabl[:, :]], dsts=[T.gath[me], T.gath[me]], alu_op=1) for e in range(8)],
+            local_sem=T.sem.sent)
+        g.wait_ge(T.sem.sent, 8)
         return
 
     g.sync.dma_start(T.xd[1 - R], T.x[:, 16 * (1 - R):16 * (1 - R) + 16]).then_inc(T.sem.ldf, 16)
     g.scalar.dma_start(T.xd[R], T.x[:, 16 * R:16 * R + 16]).then_inc(T.sem.ldo, 16)
-    for half, ld, buf, arr in ((1 - R, T.sem.ldf, T.landf, T.sem.arrf), (R, T.sem.ldo, T.lando, T.sem.arro)):
+    for half, ld, kd in ((1 - R, T.sem.ldf, FWD_CORE), (R, T.sem.ldo, RED_CORE)):
         g.wait_ge(ld, 16)
         for u in range(2):
             g.remote_dma_fused([RemoteDMATransfer(
-                dst_ids=[dst(_world(hosts[u], e, RED_CORE))], dma_engine_mask=1 << e, remote_sem=arr,
-                src=T.xd[half, u * 8 + e], dst=buf[me]) for e in range(8)], local_sem=T.sem.sent)
+                dst_ids=[dst(_world(hosts[u], e, kd))], dma_engine_mask=1 << e, remote_sem=T.sem.arr,
+                src=T.xd[half, u * 8 + e], dst=T.land[me]) for e in range(8)], local_sem=T.sem.sent)
     g.wait_ge(T.sem.gathd, 16)
     jl = (h * 8 + c) - 16 * R
     g.dma_start(T.y[:, :], T.gath[:, jl::16, :], allow_slow_non_contiguous=True).then_inc(T.sem.stored, 16)

from concourse.bass import DstId, RemoteDMATransfer

SCRATCH = {
    "xd": ("dram", [2, 16, 128, 1], "float32"),
    "land": ("dram", [16, 128, 1], "float32"),
    "cabl": ("dram", [128, 1], "float32"),
    "gath": ("dram", [16, 128, 1], "float32"),
}
SEMAPHORES = ["ldf", "ldo", "sent", "arr", "cabarr", "gathd", "stored"]

RANK_CORE, FWD_CORE, RED_CORE = 6, 7, 2


def _world(h, c, k):
    return h * 128 + c * 8 + k


def _hosts(R):
    return (0, 1) if R == 0 else (3, 2)


def rank_program(g, core, T, topo):
    h, c, k = topo.host(core), topo.chip(core), core % 8
    if c >= 8 or k not in (RANK_CORE, FWD_CORE, RED_CORE):
        return
    R = topo.rack(h)
    hosts = _hosts(R)
    me = hosts.index(h) * 8 + c

    def dst(d):
        rid, pid = topo.addr(d, core)
        return DstId(rid=rid, pnc=pid)

    landed = [T.land[s] for s in range(16)]

    if k == FWD_CORE:
        g.wait_ge(T.sem.arr, 16)
        g.remote_dma_fused([RemoteDMATransfer(
            dst_ids=[dst(_world(3 - h, c, RED_CORE))], dma_engine_mask=0xFF, remote_sem=T.sem.cabarr,
            srcs=landed, dsts=[T.cabl[:, :]], alu_op=1)], local_sem=T.sem.sent)
        g.wait_ge(T.sem.sent, 8)
        return

    if k == RED_CORE:
        g.wait_ge(T.sem.arr, 16)
        g.wait_ge(T.sem.cabarr, 8)
        g.remote_dma_fused([RemoteDMATransfer(
            dst_ids=[dst(_world(hh, e, RANK_CORE)) for hh in hosts], dma_engine_mask=1 << e, remote_sem=T.sem.gathd,
            srcs=landed + [T.cabl[:, :]], dsts=[T.gath[me], T.gath[me]], alu_op=1) for e in range(8)],
            local_sem=T.sem.sent)
        g.wait_ge(T.sem.sent, 8)
        return

    g.sync.dma_start(T.xd[1 - R], T.x[:, 16 * (1 - R):16 * (1 - R) + 16]).then_inc(T.sem.ldf, 16)
    g.scalar.dma_start(T.xd[R], T.x[:, 16 * R:16 * R + 16]).then_inc(T.sem.ldo, 16)
    for half, ld, kd in ((1 - R, T.sem.ldf, FWD_CORE), (R, T.sem.ldo, RED_CORE)):
        g.wait_ge(ld, 16)
        for u in range(2):
            g.remote_dma_fused([RemoteDMATransfer(
                dst_ids=[dst(_world(hosts[u], e, kd))], dma_engine_mask=1 << e, remote_sem=T.sem.arr,
                src=T.xd[half, u * 8 + e], dst=T.land[me]) for e in range(8)], local_sem=T.sem.sent)
    g.wait_ge(T.sem.gathd, 16)
    jl = (h * 8 + c) - 16 * R
    g.dma_start(T.y[:, :], T.gath[:, jl::16, :], allow_slow_non_contiguous=True).then_inc(T.sem.stored, 16)
    g.wait_ge(T.sem.sent, 32)
    g.wait_ge(T.sem.stored, 16)
